import numpy as np
import ml_dtypes


def mxq(x, axis, fmt="e4m3"):
    dtype, down = {"e4m3": (ml_dtypes.float8_e4m3fn, 7), "e5m2": (ml_dtypes.float8_e5m2, 14)}[fmt]
    v = np.moveaxis(np.asarray(x, np.float32).astype(ml_dtypes.bfloat16).astype(np.float64), axis, -1)
    blocks = v.reshape(v.shape[:-1] + (-1, 32))
    amax = np.abs(blocks).max(-1, keepdims=True)
    byte = np.maximum(np.where(amax > 0, np.frexp(amax)[1] - 1 + 127, 0) - down, 1)
    scale = np.exp2(byte - 127.0)
    codes = (blocks / scale).astype(np.float32).astype(dtype).astype(np.float64)
    return np.moveaxis((codes * scale).reshape(v.shape), -1, axis)


WIDE = False


def mx_kscale(k):
    if not WIDE:
        return np.ones(k)
    levels = np.array([10, -10, 5, -5, 0])
    if k % 512:
        return np.exp2(np.random.permutation(np.resize(levels, k // 32))).repeat(32)
    a = np.empty((k // 512, 16))
    for p in range(k // 512):
        a[p, :8] = np.random.permutation(np.resize(levels, 8))
        for g in range(8):
            far = levels[np.abs(levels - a[p, g]) >= 10]
            a[p, g + 8] = far[np.random.randint(len(far))]
    return np.exp2(a.ravel()).repeat(32)


def f64(x):
    return np.asarray(x).astype(np.float64)


def striped(idx):
    return np.tile(idx.reshape(-1, 16).T, (8, 1)).astype(np.uint16)


def unstriped(offs):
    return offs[:16].T.reshape(-1).astype(np.int64)


E2M1 = np.array([0.0, 0.5, 1.0, 1.5, 2.0, 3.0, 4.0, 6.0, -0.0, -0.5, -1.0, -1.5, -2.0, -3.0, -4.0, -6.0])


def pack_weight(w, fmt):
    k, n = w.shape
    w = f64(np.asarray(w, np.float32).astype(ml_dtypes.bfloat16)).reshape(k // 32, 32, n)
    amax = np.abs(w).max(1)
    if fmt == "e4m3":
        byte = np.frexp(amax)[1] - 1 + 127 - 7
    else:
        mant, ex = np.frexp(amax / 6.0)
        byte = np.where(mant > 0.5, ex, ex - 1) + 127
    byte = np.clip(np.where(amax > 0, byte, 1), 1, 254)
    scaled = (w * np.exp2(127.0 - byte)[:, None, :]).reshape(k, n).astype(np.float32)
    by_word = np.ascontiguousarray(scaled.reshape(k // 512, 128, 4, n).transpose(0, 1, 3, 2))
    if fmt == "e4m3":
        words = by_word.astype(ml_dtypes.float8_e4m3fn).view(np.uint8)
    else:
        c = by_word.astype(ml_dtypes.float4_e2m1fn).view(np.uint8) & 0xF
        words = (c[..., 0::2] | (c[..., 1::2] << 4)).reshape(k // 512, 128, 2 * n)
    return np.ascontiguousarray(words), np.ascontiguousarray(byte.astype(np.uint8).reshape(k // 512, 16, n))


def unpack_weight(words, scales, fmt):
    g, _, n = scales.shape
    words = np.ascontiguousarray(words).reshape(g, 128, n, -1)
    if fmt == "e4m3":
        vals = words.view(ml_dtypes.float8_e4m3fn).astype(np.float64)
    else:
        nib = np.empty((g, 128, n, 4), np.uint8)
        nib[..., 0::2] = words & 0xF
        nib[..., 1::2] = words >> 4
        vals = E2M1[nib]
    vals = vals * np.repeat(np.exp2(scales.astype(np.float64) - 127.0), 8, axis=1)[..., None]
    return vals.transpose(0, 1, 3, 2).reshape(g * 512, n)


def gelu(v):
    return 0.5 * v * (1.0 + np.tanh(np.sqrt(2.0 / np.pi) * (v + 0.044715 * v**3)))


K, T, S, H, T2, P = 512, 4096, 1024, 1536, 2048, 512

def setup_inputs():
    n = np.random.standard_normal
    s = mx_kscale(K)[:, None]
    u = mx_kscale(H)
    tab_words, tab_scales = pack_weight(n((K, T)) * s, "e4m3")
    w4_words, w4_scales = pack_weight(n((K, H)) * 1.8 / np.sqrt(K) / s, "e2m1")
    sign = np.random.choice([-1.0, 1.0], H)
    return {
        "tab_words": tab_words, "tab_scales": tab_scales,
        "offs": striped(np.random.permutation(T)[:S]),
        "w1": (n((K, H)) * 0.54 / np.sqrt(K) / s).astype(np.float32),
        "w4_words": w4_words, "w4_scales": w4_scales,
        "gain": (np.exp(0.2 * n(H)) * u).astype(np.float32),
        "page0": (n((H, T2)) * u[:, None]).astype(np.float32),
        "wgs": np.exp(0.3 * n((128, S))).astype(np.float32),
        "offs2": striped(np.random.permutation(T2)[:S]),
        "offs3": striped(np.random.permutation(T2)[:P]),
        "offs4": striped(np.random.permutation(T2)[:P]),
        "low": ((0.5 * n(H) - 0.3) * u).astype(np.float32),
        "d": (sign * np.random.uniform(0.6, 1.6, H) / np.sqrt(H) / u**2).astype(np.float32),
        "dv": np.exp(0.3 * n(P)).astype(np.float32),
        "sv": (0.7 * n(P)).astype(np.float32),
    }

def reference(tab_words, tab_scales, offs, w1, w4_words, w4_scales, gain, page0, wgs, offs2, offs3, offs4, low, d, dv, sv):
    v = unpack_weight(tab_words, tab_scales, "e4m3")[:, unstriped(offs)]
    w4 = unpack_weight(w4_words, w4_scales, "e2m1")
    a = mxq(f64(w1), 0, "e4m3").T @ v
    b = w4.T @ v
    h = (np.sin(a) * b + a) * f64(gain)[:, None]
    page = f64(page0).copy()
    page[:, unstriped(offs2)] = np.tile(f64(wgs), (H // 128, 1)) * h
    x1 = page[:, unstriped(offs3)]
    x2 = np.maximum(page[:, unstriped(offs4)], f64(low)[:, None]) * f64(d)[:, None]
    e = mxq(x1, 0, "e4m3").T @ mxq(x2, 0, "e4m3")
    return e * f64(dv)[None, :] + f64(sv)[:, None]

@@ -1,0 +1,307 @@
+import math
+from contextlib import ExitStack
+
+import concourse.mybir as mybir
+from concourse.masks import make_identity
+
+K, T, S, H, T2, NP = 512, 4096, 1024, 1536, 2048, 512
+FLOPS = 2 * (2 * K * H * S + H * NP * NP)
+
+F32 = mybir.dt.float32
+BF16 = mybir.dt.bfloat16
+I32 = mybir.dt.int32
+U32 = mybir.dt.uint32
+U16 = mybir.dt.uint16
+U8 = mybir.dt.uint8
+FP8X4 = mybir.dt.float8_e4m3fn_x4
+FP4X4 = mybir.dt.float4_e2m1fn_x4
+ACT = mybir.ActivationFunctionType
+ALU = mybir.AluOpType
+
+P = 128
+PACK = 4
+GROUP = P * PACK
+GROUPS = H // GROUP
+SLICES = H // P
+BANK = 512
+HALVES = S // BANK
+UNITS = SLICES * HALVES
+BLOCKS = BANK // P
+TWO_PI = 2.0 * math.pi
+TURN_OFFSET = 256.0
+
+
+def tile_list_mould_shot_match_kernel(
+    tc, tab_words, tab_scales, offs, w1, w4_words, w4_scales, gain, page0, wgs, offs2, offs3, offs4, low, d, dv, sv, out
+):
+    nc = tc.nc
+    with ExitStack() as ctx:
+        keep = ctx.enter_context(tc.tile_pool(name="keep", bufs=1))
+        work = ctx.enter_context(tc.tile_pool(name="work", bufs=2))
+        ring = ctx.enter_context(tc.tile_pool(name="ring", bufs=1))
+        psum = ctx.enter_context(tc.psum_pool(name="psum", bufs=1))
+
+        idx = keep.tile([P, S // 16], U16, name="idx")
+        idx2 = keep.tile([P, S // 16], U16, name="idx2")
+        idx3 = keep.tile([P, NP // 16], U16, name="idx3")
+        idx4 = keep.tile([P, NP // 16], U16, name="idx4")
+        tabw = keep.tile([P, T], U32, name="tabw", tag="t_tabw", align_bytes=64)
+        tabs = keep.tile([P, T], U8, name="tabs", tag="t_tabs", align_bytes=64)
+        w4w_raw = keep.tile([P, 2 * H], U8, name="w4w_raw", tag="t_w4w", align_bytes=64)
+        w4s_raw = keep.tile([P, H], U8, name="w4s_raw", tag="page1", align_bytes=64)
+        ident = keep.tile([P, P], F32, name="ident", align_bytes=64)
+        gain_sb = keep.tile([P, GROUPS, PACK], F32, name="gain_sb")
+
+        nc.gpsimd.memset(tabs[:, 0 : T // 2].bitcast(I32), 0)
+        nc.vector.memset(tabs[:, T // 2 : T].bitcast(I32), 0)
+        nc.vector.memset(w4s_raw[:].bitcast(I32), 0)
+        make_identity(nc, ident[:])
+
+        w1_rows = w1.rearrange("(p i) r -> p i r", i=PACK)
+        wgs_rows = wgs.rearrange("(q t) j -> q t j", t=PACK)
+        page_rows = page0.rearrange("(g p t) c -> g t p c", p=P, t=PACK)
+
+        w1_raw, pages = {}, {}
+
+        def load_w1(g):
+            w1_raw[g] = keep.tile([P, PACK, GROUP], F32, name="w1_raw", tag="t_w1", align_bytes=64)
+            nc.sync.dma_start(w1_raw[g][:], w1_rows[:, :, g * GROUP : (g + 1) * GROUP])
+
+        def load_page(s):
+            pages[s] = keep.tile([P, T2], F32, name="page", tag="page%d" % (s % 3), align_bytes=64)
+            nc.sync.dma_start(pages[s][:], page_rows[s // PACK, s % PACK])
+
+        nc.sync.dma_start(tabw[:].bitcast(I32), tab_words[0].rearrange("p t i -> p (t i)").bitcast(I32))
+        for q in range(4):
+            nc.sync.dma_start(
+                tabs[32 * q : 32 * q + 4, :].bitcast(I32), tab_scales[0, 4 * q : 4 * q + 4, :].bitcast(I32)
+            )
+        nc.sync.dma_start(idx[:], offs)
+        load_w1(0)
+        nc.sync.dma_start(w4w_raw[:].bitcast(I32), w4_words[0].bitcast(I32))
+        for q in range(4):
+            nc.sync.dma_start(
+                w4s_raw[32 * q : 32 * q + 4, :].bitcast(I32), w4_scales[0, 4 * q : 4 * q + 4, :].bitcast(I32)
+            )
+        nc.sync.dma_start(gain_sb[:], gain.rearrange("(g p t) -> p g t", p=P, t=PACK))
+        nc.sync.dma_start(idx2[:], offs2)
+        load_page(0)
+        nc.sync.dma_start(idx4[:], offs4)
+        nc.sync.dma_start(idx3[:], offs3)
+
+        w1_codes, w1_scales, w4w, w4s = {}, {}, {}, {}
+
+        def shared(slot, dtype, columns):
+            return ring.tile([P, columns], dtype, name="slot%d" % slot, align_bytes=64)
+
+        def quantise_w1(g, pair, rounded):
+            dst = rounded[:].rearrange("p (t m i) -> p m t i", t=2, i=PACK)
+            src = w1_raw[g][:].rearrange("p i (m t) -> p m t i", t=PACK)[:, :, 2 * pair : 2 * pair + 2, :]
+            if g == 0:
+                nc.vector.tensor_copy(dst, src)
+            else:
+                nc.scalar.copy(dst, src)
+            codes = keep.tile([P, 2 * P], U32, name="w1_codes%d%d" % (g, pair), align_bytes=64)
+            scales = keep.tile([P, 2 * P], U8, name="w1_scales%d%d" % (g, pair), align_bytes=64)
+            nc.vector.quantize_mx(out=codes[:].bitcast(FP8X4), scales=scales[:], in_=rounded[:])
+            w1_codes[g, pair], w1_scales[g, pair] = codes, scales
+
+        def deal_w4(g):
+            w4w[g] = keep.tile([P, 2 * GROUP], U8, name="w4w%d" % g, align_bytes=64)
+            w4s[g] = keep.tile([P, GROUP], U8, name="w4s%d" % g, align_bytes=64)
+            nc.vector.tensor_copy(
+                w4w[g][:].rearrange("p (t m b) -> p m t b", t=PACK, b=2),
+                w4w_raw[:, 2 * GROUP * g : 2 * GROUP * (g + 1)].rearrange("p (m t b) -> p m t b", t=PACK, b=2),
+            )
+            nc.vector.tensor_copy(
+                w4s[g][:].rearrange("p (t m) -> p m t", t=PACK),
+                w4s_raw[:, GROUP * g : GROUP * (g + 1)].rearrange("p (m t) -> p m t", t=PACK),
+            )
+
+        v_codes, v_scales = [], []
+
+        def gather_table(half):
+            entries = idx[:, half * BANK // 16 : (half + 1) * BANK // 16]
+            codes = keep.tile([P, BANK], U32, name="v_codes%d" % half, align_bytes=64)
+            scales = keep.tile([P, BANK], U8, name="v_scales%d" % half, align_bytes=64)
+            nc.vector.tensor_copy(codes[:], tabw[:].indirect(entries))
+            nc.vector.tensor_copy(scales[:], tabs[:].indirect(entries))
+            v_codes.append(codes)
+            v_scales.append(scales)
+
+        gather_table(0)
+        quantise_w1(0, 0, shared(6, BF16, 2 * P * PACK))
+        gather_table(1)
+        wgs_first = keep.tile([P, S], F32, name="wgs_first", tag="t_tabs", align_bytes=64)
+        for q in range(4):
+            nc.sync.dma_start(wgs_first[32 * q : 32 * q + 32, :], wgs_rows[:, 0, :])
+        deal_w4(0)
+        quantise_w1(0, 1, keep.tile([P, 2 * P * PACK], BF16, name="rounded", tag="page2", align_bytes=64))
+        for g in range(1, GROUPS):
+            deal_w4(g)
+        consts = keep.tile([P, 3, 16], F32, name="consts", tag="t_w4w", align_bytes=64)
+        low_sb = consts[:, 0, 0:SLICES].rearrange("p (g t) -> p g t", t=PACK)
+        d_sb = consts[:, 1, 0:SLICES].rearrange("p (g t) -> p g t", t=PACK)
+        sv_sb = consts[:, 2, 0:BLOCKS]
+        nc.sync.dma_start(low_sb, low.rearrange("(g p t) -> p g t", p=P, t=PACK))
+        nc.sync.dma_start(d_sb, d.rearrange("(g p t) -> p g t", p=P, t=PACK))
+        load_page(1)
+        wgs_rest = keep.tile([P, PACK - 1, S], F32, name="wgs_rest", tag="t_tabw", align_bytes=64)
+        for q in range(4):
+            nc.sync.dma_start(wgs_rest[32 * q : 32 * q + 32, :, :], wgs_rows[:, 1:PACK, :])
+        load_w1(1)
+        with nc.allow_non_contiguous_dma(reason="one value of sv a partition"):
+            nc.sync.dma_start(sv_sb, sv.rearrange("(b p) -> p b", p=P))
+
+        a_sb, back, a_t, prod, h_sb = {}, {}, {}, {}, {}
+        x1_planes, x2_planes, x_codes, x_scales = {}, {}, {}, {}
+
+        def block(b):
+            return slice(b * P, (b + 1) * P)
+
+        def stage_a(u):
+            s, half = divmod(u, HALVES)
+            g, t = divmod(s, PACK)
+            bank = psum.tile([P, BANK], F32, name="bank_a", bufs=2)
+            nc.tensor.matmul_mx(
+                out=bank[:],
+                lhsT=w1_codes[g, t // 2][:, block(t % 2)].bitcast(FP8X4),
+                lhsT_scale=w1_scales[g, t // 2][:, block(t % 2)],
+                rhs=v_codes[half][:].bitcast(FP8X4),
+                rhs_scale=v_scales[half][:],
+                start=True,
+                stop=True,
+            )
+            turns = work.tile([P, BANK], U32, name="turns")
+            nc.scalar.activation(turns[:], bank[:], ACT.Copy, bias=TURN_OFFSET, scale=1.0 / TWO_PI)
+            a_sb[u] = work.tile([P, BANK], F32, name="a_sb", bufs=3)
+            nc.scalar.copy(a_sb[u][:], bank[:])
+            back[u] = work.tile([P, BANK], F32, name="back", bufs=3)
+            nc.scalar.activation(back[u][:], turns[:], ACT.Copy, bias=TWO_PI * TURN_OFFSET, scale=-TWO_PI)
+
+        def stage_b(u):
+            s, half = divmod(u, HALVES)
+            g, t = divmod(s, PACK)
+            angle = psum.tile([P, BANK], F32, name="bank_sum%d" % (u % 2))
+            for b in range(BLOCKS):
+                nc.tensor.matmul(
+                    angle[:, block(b)], a_sb[u][:, block(b)], ident[:], start=True, stop=False, is_transpose=True
+                )
+                nc.tensor.matmul(
+                    angle[:, block(b)], back[u][:, block(b)], ident[:], start=False, stop=True, is_transpose=True
+                )
+            a_turned = psum.tile([P, BANK], F32, name="bank_at", bufs=2)
+            for b in range(BLOCKS):
+                nc.tensor.transpose(a_turned[:, block(b)], a_sb[u][:, block(b)], ident[:])
+            b_bank = psum.tile([P, BANK], F32, name="bank_b", bufs=2)
+            for b in range(BLOCKS):
+                nc.tensor.matmul_mx(
+                    out=b_bank[:, block(b)],
+                    lhsT=v_codes[half][:, block(b)].bitcast(FP8X4),
+                    lhsT_scale=v_scales[half][:, block(b)],
+                    rhs=w4w[g][:, 2 * P * t : 2 * P * (t + 1)].bitcast(FP4X4),
+                    rhs_scale=w4s[g][:, block(t)],
+                    start=True,
+                    stop=True,
+                )
+            sine = work.tile([P, BANK], F32, name="sine", bufs=3)
+            nc.scalar.activation(sine[:], angle[:], ACT.Sin)
+            a_t[u] = work.tile([P, BANK], F32, name="a_t", bufs=3)
+            nc.scalar.copy(a_t[u][:], a_turned[:])
+            prod[u] = shared(u % 8, F32, BANK)
+            nc.vector.tensor_tensor(prod[u][:], b_bank[:], sine[:], ALU.mult)
+
+        def stage_c(u):
+            s = u // HALVES
+            g, t = divmod(s, PACK)
+            bank = psum.tile([P, BANK], F32, name="bank_sum%d" % ((u + 1) % 2))
+            for b in range(BLOCKS):
+                nc.tensor.matmul(
+                    bank[:, block(b)], a_t[u][:, block(b)], ident[:], start=True, stop=False, is_transpose=True
+                )
+                nc.tensor.matmul(
+                    bank[:, block(b)], prod[u][:, block(b)], ident[:], start=False, stop=True, is_transpose=True
+                )
+            h_sb[u] = work.tile([P, BANK], F32, name="h_sb", bufs=3)
+            nc.scalar.activation(h_sb[u][:], bank[:], ACT.Copy, scale=gain_sb[:, g, t : t + 1])
+
+        def stage_d(u):
+            s, half = divmod(u, HALVES)
+            g, t = divmod(s, PACK)
+            cols = slice(half * BANK, (half + 1) * BANK)
+            weights = wgs_first[:, cols] if t == 0 else wgs_rest[:, t - 1, cols]
+            places = idx2[:, half * BANK // 16 : (half + 1) * BANK // 16]
+            nc.vector.tensor_tensor(pages[s][:].indirect(places), h_sb[u][:], weights, ALU.mult)
+            if half < HALVES - 1:
+                return
+            if t == 0:
+                x1_planes[g] = work.tile([P, PACK, NP], BF16, name="x1_planes", align_bytes=64)
+                x2_planes[g] = work.tile([P, PACK, NP], BF16, name="x2_planes", align_bytes=64)
+            picked = work.tile([P, NP], F32, name="picked")
+            nc.vector.tensor_copy(picked[:], pages[s][:].indirect(idx4[:]))
+            nc.vector.tensor_copy(x1_planes[g][:, t, :], pages[s][:].indirect(idx3[:]))
+            nc.vector.tensor_scalar(
+                x2_planes[g][:, t, :], picked[:], low_sb[:, g, t : t + 1], d_sb[:, g, t : t + 1], ALU.max, ALU.mult
+            )
+            if s + 2 < SLICES:
+                load_page(s + 2)
+
+        def quantise_x(g, side, piece, slot):
+            planes = (x1_planes, x2_planes)[side][g]
+            cols = slice(piece * 2 * P, (piece + 1) * 2 * P)
+            woven = shared(slot, BF16, 2 * P * PACK)
+            dst = woven[:].rearrange("p (c i t) -> p c t i", i=4, t=PACK)
+            src = planes[:, :, cols].rearrange("p t (c i) -> p c t i", i=4)
+            if g == GROUPS - 1 and side == 0:
+                nc.vector.tensor_copy(dst, src)
+            else:
+                nc.scalar.copy(dst, src)
+            if piece == 0:
+                x_codes[g, side] = keep.tile([P, NP], U32, name="x_codes%d%d" % (g, side), align_bytes=64)
+                x_scales[g, side] = keep.tile([P, NP], U8, name="x_scales%d%d" % (g, side), align_bytes=64)
+            nc.vector.quantize_mx(
+                out=x_codes[g, side][:, cols].bitcast(FP8X4), scales=x_scales[g, side][:, cols], in_=woven[:]
+            )
+
+        per_group = PACK * HALVES
+        for step in range(UNITS + 2):
+            if step < UNITS:
+                stage_a(step)
+            if 1 <= step <= UNITS:
+                stage_b(step - 1)
+            if step < 2:
+                continue
+            u = step - 2
+            stage_c(u)
+            stage_d(u)
+            g, slot = divmod(u, per_group)
+            if slot in (0, 5) and g + 1 < GROUPS:
+                quantise_w1(g + 1, slot // 5, shared(slot, BF16, 2 * P * PACK))
+                if slot == 5 and g + 2 < GROUPS:
+                    load_w1(g + 2)
+            if 1 <= slot <= 4 and g > 0:
+                quantise_x(g - 1, (slot - 1) // 2, (slot - 1) % 2, slot)
+        for side in (1, 0):
+            for piece in range(2):
+                quantise_x(GROUPS - 1, side, piece, 2 * side + piece)
+
+        dv_sb = keep.tile([P, NP], F32, name="dv_sb", tag="t_w1", align_bytes=64)
+        nc.sync.dma_start(dv_sb[:], dv.partition_broadcast(P))
+        banks = [psum.tile([P, BANK], F32, name=name, bufs=2) for name in ("bank_a", "bank_a", "bank_b", "bank_b")]
+        for g in range(GROUPS):
+            for b in range(BLOCKS):
+                nc.tensor.matmul_mx(
+                    out=banks[b][:],
+                    lhsT=x_codes[g, 0][:, block(b)].bitcast(FP8X4),
+                    lhsT_scale=x_scales[g, 0][:, block(b)],
+                    rhs=x_codes[g, 1][:].bitcast(FP8X4),
+                    rhs_scale=x_scales[g, 1][:],
+                    start=(g == 0),
+                    stop=(g == GROUPS - 1),
+                )
+        for b in range(BLOCKS):
+            scaled = work.tile([P, NP], F32, name="scaled", bufs=4)
+            nc.vector.tensor_tensor(scaled[:], banks[b][:], dv_sb[:], ALU.mult)
+            result = work.tile([P, NP], F32, name="result", bufs=4)
+            nc.scalar.activation(result[:], scaled[:], ACT.Identity, bias=sv_sb[:, b : b + 1])
+            nc.sync.dma_start(out[block(b), :], result[:])

@@ -46,12 +46,15 @@ def tile_list_mould_shot_match_kernel(
         idx3 = keep.tile([P, NP // 16], U16, name="idx3")
         idx4 = keep.tile([P, NP // 16], U16, name="idx4")
         tabw = keep.tile([P, T], U32, name="tabw", tag="t_tabw", align_bytes=64)
-        tabs = keep.tile([P, T], U8, name="tabs", tag="t_tabs", align_bytes=64)
-        w4w_raw = keep.tile([P, 2 * H], U8, name="w4w_raw", tag="t_w4w", align_bytes=64)
-        w4s_raw = keep.tile([P, H], U8, name="w4s_raw", tag="page1", align_bytes=64)
+        tabs = keep.tile([P, T], U8, name="tabs", align_bytes=64)
+        w4w_raw = keep.tile([P, 2 * H], U8, name="w4w_raw", align_bytes=64)
+        w4s_raw = keep.tile([P, H], U8, name="w4s_raw", align_bytes=64)
         ident = keep.tile([P, P], F32, name="ident", align_bytes=64)
         gain_sb = keep.tile([P, GROUPS, PACK], F32, name="gain_sb")
 
+        warm = keep.tile([P, 2], F32, name="warm")
+        nc.gpsimd.memset(warm[:, 0:1], 0.0)
+        nc.scalar.activation(warm[:, 1:2], warm[:, 0:1], ACT.Sin)
         nc.gpsimd.memset(tabs[:, 0 : T // 2].bitcast(I32), 0)
         nc.vector.memset(tabs[:, T // 2 : T].bitcast(I32), 0)
         nc.vector.memset(w4s_raw[:].bitcast(I32), 0)
@@ -64,54 +67,52 @@ def tile_list_mould_shot_match_kernel(
         w1_raw, pages = {}, {}
 
         def load_w1(g):
-            w1_raw[g] = keep.tile([P, PACK, GROUP], F32, name="w1_raw", tag="t_w1", align_bytes=64)
+            w1_raw[g] = keep.tile([P, PACK, GROUP], F32, name="w1_raw", tag="t_w1" if g else "t_page0", align_bytes=64)
             nc.sync.dma_start(w1_raw[g][:], w1_rows[:, :, g * GROUP : (g + 1) * GROUP])
 
         def load_page(s):
-            pages[s] = keep.tile([P, T2], F32, name="page", tag="page%d" % (s % 3), align_bytes=64)
+            pages[s] = keep.tile([P, T2], F32, name="page", tag="t_page%d" % (s % 2), align_bytes=64)
             nc.sync.dma_start(pages[s][:], page_rows[s // PACK, s % PACK])
 
-        nc.sync.dma_start(tabw[:].bitcast(I32), tab_words[0].rearrange("p t i -> p (t i)").bitcast(I32))
-        for q in range(4):
-            nc.sync.dma_start(
-                tabs[32 * q : 32 * q + 4, :].bitcast(I32), tab_scales[0, 4 * q : 4 * q + 4, :].bitcast(I32)
-            )
         nc.sync.dma_start(idx[:], offs)
+        nc.sync.dma_start(idx2[:], offs2)
+        nc.sync.dma_start(idx3[:], offs3)
+        nc.sync.dma_start(idx4[:], offs4)
+        nc.sync.dma_start(tabw[:].bitcast(I32), tab_words[0].rearrange("p t i -> p (t i)").bitcast(I32))
         load_w1(0)
         nc.sync.dma_start(w4w_raw[:].bitcast(I32), w4_words[0].bitcast(I32))
+        nc.sync.dma_start(gain_sb[:], gain.rearrange("(g p t) -> p g t", p=P, t=PACK))
         for q in range(4):
-            nc.sync.dma_start(
+            nc.scalar.dma_start(
+                tabs[32 * q : 32 * q + 4, :].bitcast(I32), tab_scales[0, 4 * q : 4 * q + 4, :].bitcast(I32)
+            )
+        for q in range(4):
+            nc.scalar.dma_start(
                 w4s_raw[32 * q : 32 * q + 4, :].bitcast(I32), w4_scales[0, 4 * q : 4 * q + 4, :].bitcast(I32)
             )
-        nc.sync.dma_start(gain_sb[:], gain.rearrange("(g p t) -> p g t", p=P, t=PACK))
-        nc.sync.dma_start(idx2[:], offs2)
-        load_page(0)
-        nc.sync.dma_start(idx4[:], offs4)
-        nc.sync.dma_start(idx3[:], offs3)
 
         w1_codes, w1_scales, w4w, w4s = {}, {}, {}, {}
 
         def shared(slot, dtype, columns):
             return ring.tile([P, columns], dtype, name="slot%d" % slot, align_bytes=64)
 
-        def quantise_w1(g, pair, rounded):
-            dst = rounded[:].rearrange("p (t m i) -> p m t i", t=2, i=PACK)
-            src = w1_raw[g][:].rearrange("p i (m t) -> p m t i", t=PACK)[:, :, 2 * pair : 2 * pair + 2, :]
-            if g == 0:
-                nc.vector.tensor_copy(dst, src)
-            else:
-                nc.scalar.copy(dst, src)
-            codes = keep.tile([P, 2 * P], U32, name="w1_codes%d%d" % (g, pair), align_bytes=64)
-            scales = keep.tile([P, 2 * P], U8, name="w1_scales%d%d" % (g, pair), align_bytes=64)
+        def quantise_w1(g, first, count, rounded):
+            dst = rounded[:].rearrange("p (t m i) -> p m t i", t=count, i=PACK)
+            src = w1_raw[g][:].rearrange("p i (m t) -> p m t i", t=PACK)[:, :, first : first + count, :]
+            nc.scalar.copy(dst, src)
+            codes = keep.tile([P, count * P], U32, name="w1_codes%d%d" % (g, first), align_bytes=64)
+            scales = keep.tile([P, count * P], U8, name="w1_scales%d%d" % (g, first), align_bytes=64)
             nc.vector.quantize_mx(out=codes[:].bitcast(FP8X4), scales=scales[:], in_=rounded[:])
-            w1_codes[g, pair], w1_scales[g, pair] = codes, scales
+            for n in range(count):
+                w1_codes[g, first + n] = codes[:, n * P : (n + 1) * P]
+                w1_scales[g, first + n] = scales[:, n * P : (n + 1) * P]
 
         def deal_w4(g):
-            w4w[g] = keep.tile([P, 2 * GROUP], U8, name="w4w%d" % g, align_bytes=64)
-            w4s[g] = keep.tile([P, GROUP], U8, name="w4s%d" % g, align_bytes=64)
+            w4w[g] = keep.tile([P, 2 * GROUP], U8, name="w4w", tag="t_w4w%d" % g, align_bytes=64)
+            w4s[g] = keep.tile([P, GROUP], U8, name="w4s", tag="t_w4s%d" % g, align_bytes=64)
             nc.vector.tensor_copy(
-                w4w[g][:].rearrange("p (t m b) -> p m t b", t=PACK, b=2),
-                w4w_raw[:, 2 * GROUP * g : 2 * GROUP * (g + 1)].rearrange("p (m t b) -> p m t b", t=PACK, b=2),
+                w4w[g][:].bitcast(U16).rearrange("p (t m) -> p m t", t=PACK),
+                w4w_raw[:, 2 * GROUP * g : 2 * GROUP * (g + 1)].bitcast(U16).rearrange("p (m t) -> p m t", t=PACK),
             )
             nc.vector.tensor_copy(
                 w4s[g][:].rearrange("p (t m) -> p m t", t=PACK),
@@ -122,34 +123,29 @@ def tile_list_mould_shot_match_kernel(
 
         def gather_table(half):
             entries = idx[:, half * BANK // 16 : (half + 1) * BANK // 16]
-            codes = keep.tile([P, BANK], U32, name="v_codes%d" % half, align_bytes=64)
-            scales = keep.tile([P, BANK], U8, name="v_scales%d" % half, align_bytes=64)
+            codes = keep.tile([P, BANK], U32, name="v_codes", tag="t_codes%d" % half, align_bytes=64)
+            scales = keep.tile([P, BANK], U8, name="v_scales", tag="t_scales%d" % half, align_bytes=64)
             nc.vector.tensor_copy(codes[:], tabw[:].indirect(entries))
             nc.vector.tensor_copy(scales[:], tabs[:].indirect(entries))
             v_codes.append(codes)
             v_scales.append(scales)
 
         gather_table(0)
-        quantise_w1(0, 0, shared(6, BF16, 2 * P * PACK))
+        quantise_w1(0, 0, 1, keep.tile([P, P * PACK], BF16, name="rounded", tag="t_codes1", align_bytes=64))
+        quantise_w1(0, 1, 1, keep.tile([P, P * PACK], BF16, name="rounded", tag="t_scales1", align_bytes=64))
         gather_table(1)
-        wgs_first = keep.tile([P, S], F32, name="wgs_first", tag="t_tabs", align_bytes=64)
+        deal_w4(0)
+        quantise_w1(0, 2, 2, keep.tile([P, 2 * P * PACK], BF16, name="rounded", tag="t_consts", align_bytes=64))
+        load_page(0)
+        wgs_first = keep.tile([P, S], F32, name="wgs_first", tag="t_tabw", align_bytes=64)
         for q in range(4):
             nc.sync.dma_start(wgs_first[32 * q : 32 * q + 32, :], wgs_rows[:, 0, :])
-        deal_w4(0)
-        quantise_w1(0, 1, keep.tile([P, 2 * P * PACK], BF16, name="rounded", tag="page2", align_bytes=64))
-        for g in range(1, GROUPS):
-            deal_w4(g)
-        consts = keep.tile([P, 3, 16], F32, name="consts", tag="t_w4w", align_bytes=64)
+        consts = keep.tile([P, 3, 16], F32, name="consts", tag="t_consts", align_bytes=64)
         low_sb = consts[:, 0, 0:SLICES].rearrange("p (g t) -> p g t", t=PACK)
         d_sb = consts[:, 1, 0:SLICES].rearrange("p (g t) -> p g t", t=PACK)
         sv_sb = consts[:, 2, 0:BLOCKS]
         nc.sync.dma_start(low_sb, low.rearrange("(g p t) -> p g t", p=P, t=PACK))
         nc.sync.dma_start(d_sb, d.rearrange("(g p t) -> p g t", p=P, t=PACK))
-        load_page(1)
-        wgs_rest = keep.tile([P, PACK - 1, S], F32, name="wgs_rest", tag="t_tabw", align_bytes=64)
-        for q in range(4):
-            nc.sync.dma_start(wgs_rest[32 * q : 32 * q + 32, :, :], wgs_rows[:, 1:PACK, :])
-        load_w1(1)
         with nc.allow_non_contiguous_dma(reason="one value of sv a partition"):
             nc.sync.dma_start(sv_sb, sv.rearrange("(b p) -> p b", p=P))
 
@@ -159,30 +155,104 @@ def tile_list_mould_shot_match_kernel(
         def block(b):
             return slice(b * P, (b + 1) * P)
 
+        def lag(u):
+            return 1 if u < 6 else 2
+
+        early_tags = {
+            ("turns", 0): "t_w4w1",
+            ("turns", 1): "t_w4w1",
+            ("back", 0): "t_w4s1",
+            ("a_sb", 1): "t_w4w2",
+            ("back", 1): "t_w4s2",
+            ("a_sb", 0): "t_wgs",
+            ("sine", 0): "t_page1",
+            ("h_sb", 0): "t_w1",
+            ("sine", 2): "t_h1",
+            ("h_sb", 1): "t_h1",
+        }
+
+        def step_tile(name, u, dtype):
+            if (name, u) in early_tags:
+                return keep.tile([P, BANK], dtype, name=name, tag=early_tags[name, u], align_bytes=64)
+            return work.tile([P, BANK], dtype, name=name, bufs=3)
+
+        wgs_later = []
+
+        def late_loads():
+            for g in range(1, GROUPS):
+                deal_w4(g)
+            wgs_rest = keep.tile([P, PACK - 1, S], F32, name="wgs_rest", tag="t_wgs", align_bytes=64)
+            for q in range(4):
+                nc.sync.dma_start(wgs_rest[32 * q : 32 * q + 32, :, :], wgs_rows[:, 1:PACK, :])
+            wgs_later.append(wgs_rest)
+            load_page(1)
+            load_w1(1)
+
+        direct_a = {}
+
+        def direct_product(u):
+            gain_col = gain_sb[:, 0, 0:1]
+            direct_a[u] = psum.tile([P, BANK], F32, name="bank_sum%d" % u)
+            nc.tensor.matmul_mx(
+                out=direct_a[u][:],
+                lhsT=w1_codes[0, 0].bitcast(FP8X4),
+                lhsT_scale=w1_scales[0, 0],
+                rhs=v_codes[u][:].bitcast(FP8X4),
+                rhs_scale=v_scales[u][:],
+                start=True,
+                stop=True,
+            )
+            b_bank = psum.tile([P, BANK], F32, name="bank_b", bufs=2)
+            nc.tensor.matmul_mx(
+                out=b_bank[:],
+                lhsT=w4w[0][:, 0 : 2 * P].bitcast(FP4X4),
+                lhsT_scale=w4s[0][:, block(0)],
+                rhs=v_codes[u][:].bitcast(FP8X4),
+                rhs_scale=v_scales[u][:],
+                start=True,
+                stop=True,
+            )
+            turns = step_tile("turns", u, U32)
+            nc.scalar.activation(turns[:], direct_a[u][:], ACT.Copy, bias=TURN_OFFSET, scale=1.0 / TWO_PI)
+            back[u] = step_tile("back", u, F32)
+            nc.scalar.activation(back[u][:], turns[:], ACT.Copy, bias=TWO_PI * TURN_OFFSET, scale=-TWO_PI)
+            angle = step_tile("a_sb", u, F32)
+            nc.vector.tensor_tensor(angle[:], direct_a[u][:], back[u][:], ALU.add)
+            sine = step_tile("sine", u, F32)
+            nc.scalar.activation(sine[:], angle[:], ACT.Sin)
+            prod[u] = shared(u, F32, BANK)
+            nc.vector.scalar_tensor_tensor(prod[u][:], b_bank[:], gain_col, sine[:], ALU.mult, ALU.mult)
+
+        def direct_sum(u):
+            h_sb[u] = step_tile("h_sb", u, F32)
+            nc.vector.scalar_tensor_tensor(
+                h_sb[u][:], direct_a[u][:], gain_sb[:, 0, 0:1], prod[u][:], ALU.mult, ALU.add
+            )
+
         def stage_a(u):
             s, half = divmod(u, HALVES)
             g, t = divmod(s, PACK)
             bank = psum.tile([P, BANK], F32, name="bank_a", bufs=2)
             nc.tensor.matmul_mx(
                 out=bank[:],
-                lhsT=w1_codes[g, t // 2][:, block(t % 2)].bitcast(FP8X4),
-                lhsT_scale=w1_scales[g, t // 2][:, block(t % 2)],
+                lhsT=w1_codes[g, t].bitcast(FP8X4),
+                lhsT_scale=w1_scales[g, t],
                 rhs=v_codes[half][:].bitcast(FP8X4),
                 rhs_scale=v_scales[half][:],
                 start=True,
                 stop=True,
             )
-            turns = work.tile([P, BANK], U32, name="turns")
+            turns = step_tile("turns", u, U32)
             nc.scalar.activation(turns[:], bank[:], ACT.Copy, bias=TURN_OFFSET, scale=1.0 / TWO_PI)
-            a_sb[u] = work.tile([P, BANK], F32, name="a_sb", bufs=3)
+            a_sb[u] = step_tile("a_sb", u, F32)
             nc.scalar.copy(a_sb[u][:], bank[:])
-            back[u] = work.tile([P, BANK], F32, name="back", bufs=3)
+            back[u] = step_tile("back", u, F32)
             nc.scalar.activation(back[u][:], turns[:], ACT.Copy, bias=TWO_PI * TURN_OFFSET, scale=-TWO_PI)
 
         def stage_b(u):
             s, half = divmod(u, HALVES)
             g, t = divmod(s, PACK)
-            angle = psum.tile([P, BANK], F32, name="bank_sum%d" % (u % 2))
+            angle = psum.tile([P, BANK], F32, name="bank_sum%d" % (u % 3))
             for b in range(BLOCKS):
                 nc.tensor.matmul(
                     angle[:, block(b)], a_sb[u][:, block(b)], ident[:], start=True, stop=False, is_transpose=True
@@ -190,7 +260,7 @@ def tile_list_mould_shot_match_kernel(
                 nc.tensor.matmul(
                     angle[:, block(b)], back[u][:, block(b)], ident[:], start=False, stop=True, is_transpose=True
                 )
-            a_turned = psum.tile([P, BANK], F32, name="bank_at", bufs=2)
+            a_turned = psum.tile([P, BANK], F32, name="bank_at")
             for b in range(BLOCKS):
                 nc.tensor.transpose(a_turned[:, block(b)], a_sb[u][:, block(b)], ident[:])
             b_bank = psum.tile([P, BANK], F32, name="bank_b", bufs=2)
@@ -204,9 +274,9 @@ def tile_list_mould_shot_match_kernel(
                     start=True,
                     stop=True,
                 )
-            sine = work.tile([P, BANK], F32, name="sine", bufs=3)
+            sine = step_tile("sine", u, F32)
             nc.scalar.activation(sine[:], angle[:], ACT.Sin)
-            a_t[u] = work.tile([P, BANK], F32, name="a_t", bufs=3)
+            a_t[u] = work.tile([P, BANK], F32, name="a_t", bufs=4)
             nc.scalar.copy(a_t[u][:], a_turned[:])
             prod[u] = shared(u % 8, F32, BANK)
             nc.vector.tensor_tensor(prod[u][:], b_bank[:], sine[:], ALU.mult)
@@ -214,7 +284,7 @@ def tile_list_mould_shot_match_kernel(
         def stage_c(u):
             s = u // HALVES
             g, t = divmod(s, PACK)
-            bank = psum.tile([P, BANK], F32, name="bank_sum%d" % ((u + 1) % 2))
+            bank = psum.tile([P, BANK], F32, name="bank_sum%d" % ((u + lag(u)) % 3))
             for b in range(BLOCKS):
                 nc.tensor.matmul(
                     bank[:, block(b)], a_t[u][:, block(b)], ident[:], start=True, stop=False, is_transpose=True
@@ -222,14 +292,14 @@ def tile_list_mould_shot_match_kernel(
                 nc.tensor.matmul(
                     bank[:, block(b)], prod[u][:, block(b)], ident[:], start=False, stop=True, is_transpose=True
                 )
-            h_sb[u] = work.tile([P, BANK], F32, name="h_sb", bufs=3)
+            h_sb[u] = step_tile("h_sb", u, F32)
             nc.scalar.activation(h_sb[u][:], bank[:], ACT.Copy, scale=gain_sb[:, g, t : t + 1])
 
         def stage_d(u):
             s, half = divmod(u, HALVES)
             g, t = divmod(s, PACK)
             cols = slice(half * BANK, (half + 1) * BANK)
-            weights = wgs_first[:, cols] if t == 0 else wgs_rest[:, t - 1, cols]
+            weights = wgs_first[:, cols] if t == 0 else wgs_later[0][:, t - 1, cols]
             places = idx2[:, half * BANK // 16 : (half + 1) * BANK // 16]
             nc.vector.tensor_tensor(pages[s][:].indirect(places), h_sb[u][:], weights, ALU.mult)
             if half < HALVES - 1:
@@ -264,23 +334,34 @@ def tile_list_mould_shot_match_kernel(
             )
 
         per_group = PACK * HALVES
-        for step in range(UNITS + 2):
-            if step < UNITS:
-                stage_a(step)
-            if 1 <= step <= UNITS:
-                stage_b(step - 1)
-            if step < 2:
-                continue
-            u = step - 2
-            stage_c(u)
+        def finish(u):
             stage_d(u)
             g, slot = divmod(u, per_group)
-            if slot in (0, 5) and g + 1 < GROUPS:
-                quantise_w1(g + 1, slot // 5, shared(slot, BF16, 2 * P * PACK))
+            if slot in (3 if g == 0 else 0, 5) and g + 1 < GROUPS:
+                quantise_w1(g + 1, 2 * (slot // 5), 2, shared(slot, BF16, 2 * P * PACK))
                 if slot == 5 and g + 2 < GROUPS:
                     load_w1(g + 2)
             if 1 <= slot <= 4 and g > 0:
                 quantise_x(g - 1, (slot - 1) // 2, (slot - 1) % 2, slot)
+
+        direct_product(0)
+        direct_sum(0)
+        direct_product(1)
+        finish(0)
+        late_loads()
+        stage_a(2)
+        for step in range(3, UNITS + 3):
+            if step < UNITS:
+                stage_a(step)
+            if step <= UNITS:
+                stage_b(step - 1)
+            if step == 3:
+                direct_sum(1)
+                finish(1)
+            for u in range(2, UNITS):
+                if u + lag(u) + 1 == step:
+                    stage_c(u)
+                    finish(u)
         for side in (1, 0):
             for piece in range(2):
                 quantise_x(GROUPS - 1, side, piece, 2 * side + piece)

import math
from contextlib import ExitStack

import concourse.mybir as mybir
from concourse.masks import make_identity

K, T, S, H, T2, NP = 512, 4096, 1024, 1536, 2048, 512
FLOPS = 2 * (2 * K * H * S + H * NP * NP)

F32 = mybir.dt.float32
BF16 = mybir.dt.bfloat16
I32 = mybir.dt.int32
U32 = mybir.dt.uint32
U16 = mybir.dt.uint16
U8 = mybir.dt.uint8
FP8X4 = mybir.dt.float8_e4m3fn_x4
FP4X4 = mybir.dt.float4_e2m1fn_x4
ACT = mybir.ActivationFunctionType
ALU = mybir.AluOpType

P = 128
PACK = 4
GROUP = P * PACK
GROUPS = H // GROUP
SLICES = H // P
BANK = 512
HALVES = S // BANK
UNITS = SLICES * HALVES
BLOCKS = BANK // P
TWO_PI = 2.0 * math.pi
TURN_OFFSET = 256.0


def tile_list_mould_shot_match_kernel(
    tc, tab_words, tab_scales, offs, w1, w4_words, w4_scales, gain, page0, wgs, offs2, offs3, offs4, low, d, dv, sv, out
):
    nc = tc.nc
    with ExitStack() as ctx:
        keep = ctx.enter_context(tc.tile_pool(name="keep", bufs=1))
        work = ctx.enter_context(tc.tile_pool(name="work", bufs=2))
        ring = ctx.enter_context(tc.tile_pool(name="ring", bufs=1))
        psum = ctx.enter_context(tc.psum_pool(name="psum", bufs=1))

        idx = keep.tile([P, S // 16], U16, name="idx")
        idx2 = keep.tile([P, S // 16], U16, name="idx2")
        idx3 = keep.tile([P, NP // 16], U16, name="idx3")
        idx4 = keep.tile([P, NP // 16], U16, name="idx4")
        tabw = keep.tile([P, T], U32, name="tabw", tag="t_tabw", align_bytes=64)
        tabs = keep.tile([P, T], U8, name="tabs", align_bytes=64)
        w4w_raw = keep.tile([P, 2 * H], U8, name="w4w_raw", align_bytes=64)
        w4s_raw = keep.tile([P, H], U8, name="w4s_raw", align_bytes=64)
        ident = keep.tile([P, P], F32, name="ident", align_bytes=64)
        gain_sb = keep.tile([P, GROUPS, PACK], F32, name="gain_sb")

        warm = keep.tile([P, 2], F32, name="warm")
        nc.gpsimd.memset(warm[:, 0:1], 0.0)
        nc.scalar.activation(warm[:, 1:2], warm[:, 0:1], ACT.Sin)
        nc.gpsimd.memset(tabs[:, 0 : T // 2].bitcast(I32), 0)
        nc.vector.memset(tabs[:, T // 2 : T].bitcast(I32), 0)
        nc.vector.memset(w4s_raw[:].bitcast(I32), 0)
        make_identity(nc, ident[:])

        w1_rows = w1.rearrange("(p i) r -> p i r", i=PACK)
        wgs_rows = wgs.rearrange("(q t) j -> q t j", t=PACK)
        page_rows = page0.rearrange("(g p t) c -> g t p c", p=P, t=PACK)

        w1_raw, pages = {}, {}

        def load_w1(g):
            w1_raw[g] = keep.tile([P, PACK, GROUP], F32, name="w1_raw", tag="t_w1" if g else "t_page0", align_bytes=64)
            nc.sync.dma_start(w1_raw[g][:], w1_rows[:, :, g * GROUP : (g + 1) * GROUP])

        def load_page(s):
            pages[s] = keep.tile([P, T2], F32, name="page", tag="t_page%d" % (s % 2), align_bytes=64)
            nc.sync.dma_start(pages[s][:], page_rows[s // PACK, s % PACK])

        nc.sync.dma_start(idx[:], offs)
        nc.sync.dma_start(idx2[:], offs2)
        nc.sync.dma_start(idx3[:], offs3)
        nc.sync.dma_start(idx4[:], offs4)
        nc.sync.dma_start(tabw[:].bitcast(I32), tab_words[0].rearrange("p t i -> p (t i)").bitcast(I32))
        load_w1(0)
        nc.sync.dma_start(w4w_raw[:].bitcast(I32), w4_words[0].bitcast(I32))
        nc.sync.dma_start(gain_sb[:], gain.rearrange("(g p t) -> p g t", p=P, t=PACK))
        for q in range(4):
            nc.scalar.dma_start(
                tabs[32 * q : 32 * q + 4, :].bitcast(I32), tab_scales[0, 4 * q : 4 * q + 4, :].bitcast(I32)
            )
        for q in range(4):
            nc.scalar.dma_start(
                w4s_raw[32 * q : 32 * q + 4, :].bitcast(I32), w4_scales[0, 4 * q : 4 * q + 4, :].bitcast(I32)
            )

        w1_codes, w1_scales, w4w, w4s = {}, {}, {}, {}

        def shared(slot, dtype, columns):
            return ring.tile([P, columns], dtype, name="slot%d" % slot, align_bytes=64)

        def quantise_w1(g, first, count, rounded):
            dst = rounded[:].rearrange("p (t m i) -> p m t i", t=count, i=PACK)
            src = w1_raw[g][:].rearrange("p i (m t) -> p m t i", t=PACK)[:, :, first : first + count, :]
            nc.scalar.copy(dst, src)
            codes = keep.tile([P, count * P], U32, name="w1_codes%d%d" % (g, first), align_bytes=64)
            scales = keep.tile([P, count * P], U8, name="w1_scales%d%d" % (g, first), align_bytes=64)
            nc.vector.quantize_mx(out=codes[:].bitcast(FP8X4), scales=scales[:], in_=rounded[:])
            for n in range(count):
                w1_codes[g, first + n] = codes[:, n * P : (n + 1) * P]
                w1_scales[g, first + n] = scales[:, n * P : (n + 1) * P]

        def deal_w4(g):
            w4w[g] = keep.tile([P, 2 * GROUP], U8, name="w4w", tag="t_w4w%d" % g, align_bytes=64)
            w4s[g] = keep.tile([P, GROUP], U8, name="w4s", tag="t_w4s%d" % g, align_bytes=64)
            nc.vector.tensor_copy(
                w4w[g][:].bitcast(U16).rearrange("p (t m) -> p m t", t=PACK),
                w4w_raw[:, 2 * GROUP * g : 2 * GROUP * (g + 1)].bitcast(U16).rearrange("p (m t) -> p m t", t=PACK),
            )
            nc.vector.tensor_copy(
                w4s[g][:].rearrange("p (t m) -> p m t", t=PACK),
                w4s_raw[:, GROUP * g : GROUP * (g + 1)].rearrange("p (m t) -> p m t", t=PACK),
            )

        v_codes, v_scales = [], []

        def gather_table(half):
            entries = idx[:, half * BANK // 16 : (half + 1) * BANK // 16]
            codes = keep.tile([P, BANK], U32, name="v_codes", tag="t_codes%d" % half, align_bytes=64)
            scales = keep.tile([P, BANK], U8, name="v_scales", tag="t_scales%d" % half, align_bytes=64)
            nc.vector.tensor_copy(codes[:], tabw[:].indirect(entries))
            nc.vector.tensor_copy(scales[:], tabs[:].indirect(entries))
            v_codes.append(codes)
            v_scales.append(scales)

        gather_table(0)
        quantise_w1(0, 0, 1, keep.tile([P, P * PACK], BF16, name="rounded", tag="t_codes1", align_bytes=64))
        quantise_w1(0, 1, 1, keep.tile([P, P * PACK], BF16, name="rounded", tag="t_scales1", align_bytes=64))
        gather_table(1)
        deal_w4(0)
        quantise_w1(0, 2, 2, keep.tile([P, 2 * P * PACK], BF16, name="rounded", tag="t_consts", align_bytes=64))
        load_page(0)
        wgs_first = keep.tile([P, S], F32, name="wgs_first", tag="t_tabw", align_bytes=64)
        for q in range(4):
            nc.sync.dma_start(wgs_first[32 * q : 32 * q + 32, :], wgs_rows[:, 0, :])
        consts = keep.tile([P, 3, 16], F32, name="consts", tag="t_consts", align_bytes=64)
        low_sb = consts[:, 0, 0:SLICES].rearrange("p (g t) -> p g t", t=PACK)
        d_sb = consts[:, 1, 0:SLICES].rearrange("p (g t) -> p g t", t=PACK)
        sv_sb = consts[:, 2, 0:BLOCKS]
        nc.sync.dma_start(low_sb, low.rearrange("(g p t) -> p g t", p=P, t=PACK))
        nc.sync.dma_start(d_sb, d.rearrange("(g p t) -> p g t", p=P, t=PACK))
        with nc.allow_non_contiguous_dma(reason="one value of sv a partition"):
            nc.sync.dma_start(sv_sb, sv.rearrange("(b p) -> p b", p=P))

        a_sb, back, a_t, prod, h_sb = {}, {}, {}, {}, {}
        x1_planes, x2_planes, x_codes, x_scales = {}, {}, {}, {}

        def block(b):
            return slice(b * P, (b + 1) * P)

        def lag(u):
            return 1 if u < 6 else 2

        early_tags = {
            ("turns", 0): "t_w4w1",
            ("turns", 1): "t_w4w1",
            ("back", 0): "t_w4s1",
            ("a_sb", 1): "t_w4w2",
            ("back", 1): "t_w4s2",
            ("a_sb", 0): "t_wgs",
            ("sine", 0): "t_page1",
            ("h_sb", 0): "t_w1",
            ("sine", 2): "t_h1",
            ("h_sb", 1): "t_h1",
        }

        def step_tile(name, u, dtype):
            if (name, u) in early_tags:
                return keep.tile([P, BANK], dtype, name=name, tag=early_tags[name, u], align_bytes=64)
            return work.tile([P, BANK], dtype, name=name, bufs=3)

        wgs_later = []

        def late_loads():
            for g in range(1, GROUPS):
                deal_w4(g)
            wgs_rest = keep.tile([P, PACK - 1, S], F32, name="wgs_rest", tag="t_wgs", align_bytes=64)
            for q in range(4):
                nc.sync.dma_start(wgs_rest[32 * q : 32 * q + 32, :, :], wgs_rows[:, 1:PACK, :])
            wgs_later.append(wgs_rest)
            load_page(1)
            load_w1(1)

        direct_a = {}

        def direct_product(u):
            gain_col = gain_sb[:, 0, 0:1]
            direct_a[u] = psum.tile([P, BANK], F32, name="bank_sum%d" % u)
            nc.tensor.matmul_mx(
                out=direct_a[u][:],
                lhsT=w1_codes[0, 0].bitcast(FP8X4),
                lhsT_scale=w1_scales[0, 0],
                rhs=v_codes[u][:].bitcast(FP8X4),
                rhs_scale=v_scales[u][:],
                start=True,
                stop=True,
            )
            b_bank = psum.tile([P, BANK], F32, name="bank_b", bufs=2)
            nc.tensor.matmul_mx(
                out=b_bank[:],
                lhsT=w4w[0][:, 0 : 2 * P].bitcast(FP4X4),
                lhsT_scale=w4s[0][:, block(0)],
                rhs=v_codes[u][:].bitcast(FP8X4),
                rhs_scale=v_scales[u][:],
                start=True,
                stop=True,
            )
            turns = step_tile("turns", u, U32)
            nc.scalar.activation(turns[:], direct_a[u][:], ACT.Copy, bias=TURN_OFFSET, scale=1.0 / TWO_PI)
            back[u] = step_tile("back", u, F32)
            nc.scalar.activation(back[u][:], turns[:], ACT.Copy, bias=TWO_PI * TURN_OFFSET, scale=-TWO_PI)
            angle = step_tile("a_sb", u, F32)
            nc.vector.tensor_tensor(angle[:], direct_a[u][:], back[u][:], ALU.add)
            sine = step_tile("sine", u, F32)
            nc.scalar.activation(sine[:], angle[:], ACT.Sin)
            prod[u] = shared(u, F32, BANK)
            nc.vector.scalar_tensor_tensor(prod[u][:], b_bank[:], gain_col, sine[:], ALU.mult, ALU.mult)

        def direct_sum(u):
            h_sb[u] = step_tile("h_sb", u, F32)
            nc.vector.scalar_tensor_tensor(
                h_sb[u][:], direct_a[u][:], gain_sb[:, 0, 0:1], prod[u][:], ALU.mult, ALU.add
            )

        def stage_a(u):
            s, half = divmod(u, HALVES)
            g, t = divmod(s, PACK)
            bank = psum.tile([P, BANK], F32, name="bank_a", bufs=2)
            nc.tensor.matmul_mx(
                out=bank[:],
                lhsT=w1_codes[g, t].bitcast(FP8X4),
                lhsT_scale=w1_scales[g, t],
                rhs=v_codes[half][:].bitcast(FP8X4),
                rhs_scale=v_scales[half][:],
                start=True,
                stop=True,
            )
            turns = step_tile("turns", u, U32)
            nc.scalar.activation(turns[:], bank[:], ACT.Copy, bias=TURN_OFFSET, scale=1.0 / TWO_PI)
            a_sb[u] = step_tile("a_sb", u, F32)
            nc.scalar.copy(a_sb[u][:], bank[:])
            back[u] = step_tile("back", u, F32)
            nc.scalar.activation(back[u][:], turns[:], ACT.Copy, bias=TWO_PI * TURN_OFFSET, scale=-TWO_PI)

        def stage_b(u):
            s, half = divmod(u, HALVES)
            g, t = divmod(s, PACK)
            angle = psum.tile([P, BANK], F32, name="bank_sum%d" % (u % 3))
            for b in range(BLOCKS):
                nc.tensor.matmul(
                    angle[:, block(b)], a_sb[u][:, block(b)], ident[:], start=True, stop=False, is_transpose=True
                )
                nc.tensor.matmul(
                    angle[:, block(b)], back[u][:, block(b)], ident[:], start=False, stop=True, is_transpose=True
                )
            a_turned = psum.tile([P, BANK], F32, name="bank_at")
            for b in range(BLOCKS):
                nc.tensor.transpose(a_turned[:, block(b)], a_sb[u][:, block(b)], ident[:])
            b_bank = psum.tile([P, BANK], F32, name="bank_b", bufs=2)
            for b in range(BLOCKS):
                nc.tensor.matmul_mx(
                    out=b_bank[:, block(b)],
                    lhsT=v_codes[half][:, block(b)].bitcast(FP8X4),
                    lhsT_scale=v_scales[half][:, block(b)],
                    rhs=w4w[g][:, 2 * P * t : 2 * P * (t + 1)].bitcast(FP4X4),
                    rhs_scale=w4s[g][:, block(t)],
                    start=True,
                    stop=True,
                )
            sine = step_tile("sine", u, F32)
            nc.scalar.activation(sine[:], angle[:], ACT.Sin)
            a_t[u] = work.tile([P, BANK], F32, name="a_t", bufs=4)
            nc.scalar.copy(a_t[u][:], a_turned[:])
            prod[u] = shared(u % 8, F32, BANK)
            nc.vector.tensor_tensor(prod[u][:], b_bank[:], sine[:], ALU.mult)

        def stage_c(u):
            s = u // HALVES
            g, t = divmod(s, PACK)
            bank = psum.tile([P, BANK], F32, name="bank_sum%d" % ((u + lag(u)) % 3))
            for b in range(BLOCKS):
                nc.tensor.matmul(
                    bank[:, block(b)], a_t[u][:, block(b)], ident[:], start=True, stop=False, is_transpose=True
                )
                nc.tensor.matmul(
                    bank[:, block(b)], prod[u][:, block(b)], ident[:], start=False, stop=True, is_transpose=True
                )
            h_sb[u] = step_tile("h_sb", u, F32)
            nc.scalar.activation(h_sb[u][:], bank[:], ACT.Copy, scale=gain_sb[:, g, t : t + 1])

        def stage_d(u):
            s, half = divmod(u, HALVES)
            g, t = divmod(s, PACK)
            cols = slice(half * BANK, (half + 1) * BANK)
            weights = wgs_first[:, cols] if t == 0 else wgs_later[0][:, t - 1, cols]
            places = idx2[:, half * BANK // 16 : (half + 1) * BANK // 16]
            nc.vector.tensor_tensor(pages[s][:].indirect(places), h_sb[u][:], weights, ALU.mult)
            if half < HALVES - 1:
                return
            if t == 0:
                x1_planes[g] = work.tile([P, PACK, NP], BF16, name="x1_planes", align_bytes=64)
                x2_planes[g] = work.tile([P, PACK, NP], BF16, name="x2_planes", align_bytes=64)
            picked = work.tile([P, NP], F32, name="picked")
            nc.vector.tensor_copy(picked[:], pages[s][:].indirect(idx4[:]))
            nc.vector.tensor_copy(x1_planes[g][:, t, :], pages[s][:].indirect(idx3[:]))
            nc.vector.tensor_scalar(
                x2_planes[g][:, t, :], picked[:], low_sb[:, g, t : t + 1], d_sb[:, g, t : t + 1], ALU.max, ALU.mult
            )
            if s + 2 < SLICES:
                load_page(s + 2)

        def quantise_x(g, side, piece, slot):
            planes = (x1_planes, x2_planes)[side][g]
            cols = slice(piece * 2 * P, (piece + 1) * 2 * P)
            woven = shared(slot, BF16, 2 * P * PACK)
            dst = woven[:].rearrange("p (c i t) -> p c t i", i=4, t=PACK)
            src = planes[:, :, cols].rearrange("p t (c i) -> p c t i", i=4)
            if g == GROUPS - 1 and side == 0:
                nc.vector.tensor_copy(dst, src)
            else:
                nc.scalar.copy(dst, src)
            if piece == 0:
                x_codes[g, side] = keep.tile([P, NP], U32, name="x_codes%d%d" % (g, side), align_bytes=64)
                x_scales[g, side] = keep.tile([P, NP], U8, name="x_scales%d%d" % (g, side), align_bytes=64)
            nc.vector.quantize_mx(
                out=x_codes[g, side][:, cols].bitcast(FP8X4), scales=x_scales[g, side][:, cols], in_=woven[:]
            )

        per_group = PACK * HALVES
        def finish(u):
            stage_d(u)
            g, slot = divmod(u, per_group)
            if slot in (3 if g == 0 else 0, 5) and g + 1 < GROUPS:
                quantise_w1(g + 1, 2 * (slot // 5), 2, shared(slot, BF16, 2 * P * PACK))
                if slot == 5 and g + 2 < GROUPS:
                    load_w1(g + 2)
            if 1 <= slot <= 4 and g > 0:
                quantise_x(g - 1, (slot - 1) // 2, (slot - 1) % 2, slot)

        direct_product(0)
        direct_sum(0)
        direct_product(1)
        finish(0)
        late_loads()
        stage_a(2)
        for step in range(3, UNITS + 3):
            if step < UNITS:
                stage_a(step)
            if step <= UNITS:
                stage_b(step - 1)
            if step == 3:
                direct_sum(1)
                finish(1)
            for u in range(2, UNITS):
                if u + lag(u) + 1 == step:
                    stage_c(u)
                    finish(u)
        for side in (1, 0):
            for piece in range(2):
                quantise_x(GROUPS - 1, side, piece, 2 * side + piece)

        dv_sb = keep.tile([P, NP], F32, name="dv_sb", tag="t_w1", align_bytes=64)
        nc.sync.dma_start(dv_sb[:], dv.partition_broadcast(P))
        banks = [psum.tile([P, BANK], F32, name=name, bufs=2) for name in ("bank_a", "bank_a", "bank_b", "bank_b")]
        for g in range(GROUPS):
            for b in range(BLOCKS):
                nc.tensor.matmul_mx(
                    out=banks[b][:],
                    lhsT=x_codes[g, 0][:, block(b)].bitcast(FP8X4),
                    lhsT_scale=x_scales[g, 0][:, block(b)],
                    rhs=x_codes[g, 1][:].bitcast(FP8X4),
                    rhs_scale=x_scales[g, 1][:],
                    start=(g == 0),
                    stop=(g == GROUPS - 1),
                )
        for b in range(BLOCKS):
            scaled = work.tile([P, NP], F32, name="scaled", bufs=4)
            nc.vector.tensor_tensor(scaled[:], banks[b][:], dv_sb[:], ALU.mult)
            result = work.tile([P, NP], F32, name="result", bufs=4)
            nc.scalar.activation(result[:], scaled[:], ACT.Identity, bias=sv_sb[:, b : b + 1])
            nc.sync.dma_start(out[block(b), :], result[:])
